import numpy as np, ml_dtypes
CORES = [16,18,20,22]
N = 4
import mx_ref
BF = ml_dtypes.bfloat16
def entries(a):
    return np.ascontiguousarray(a.T).reshape(-1)
def table(e):
    return np.ascontiguousarray(np.reshape(e, (-1, 16)).T).astype(np.int32)
def cut(t, i, w=512):
    return t[:, w * i:w * i + w]
def f(rng, *shape):
    return mx_ref.flush((rng.standard_normal(shape, dtype=np.float32) * np.exp2(rng.integers(-2, 3, shape[:-1] + (1,)))).astype(BF))
def wide(rng, *shape, cols=0):
    v = rng.standard_normal(shape, dtype=np.float32) * np.exp2(rng.integers(-12, 13, shape)).astype(np.float32)
    if cols: v *= np.repeat(np.exp2(rng.integers(-cols, cols + 1, shape[:-2] + (1, shape[-1] // 4))) * (rng.random(shape[:-2] + (1, shape[-1] // 4)) > 0.0625), 4, axis=-1).astype(np.float32)
    return mx_ref.flush(v.astype(BF))
SH, CH, R = 256, 64, 3
def lists(rng, how=""):
    o = []
    for q in range(N):
        p = rng.permutation(SH); h = int(rng.integers(0, 2)); e = []
        for t in range(R):
            if how == "same": v = p[:CH]
            elif how == "apart": v = p[CH * t:CH * t + CH]
            elif how == "ends": v = np.arange(CH) + (SH - CH) * ((h + t) % 2)
            elif how == "pairs": v = p[CH:2 * CH] if t >= 2 - h else p[:CH]
            else: v = rng.permutation(SH)[:CH]
            e.append(rng.permutation(v))
        o.append(table(np.concatenate(e)))
    return np.stack(o)
def fit(v):
    v = np.array(v); v[np.abs(v.astype(np.float32)) < np.float32(2.0 ** -30)] = 0
    return v
def setup_inputs(rng):
    return {"x": f(rng, N, 128, 512 * (R + 1)), "wm": f(rng, N, 128, 4 * SH), "dl": f(rng, N, 128, 4 * R * CH), "ix": lists(rng)}
def setup_inputs_same(rng):
    d = setup_inputs(rng); d["ix"] = lists(rng, "same"); return d
def setup_inputs_apart(rng):
    d = setup_inputs(rng); d["ix"] = lists(rng, "apart"); return d
def setup_inputs_ends(rng):
    d = setup_inputs(rng); d["ix"] = lists(rng, "ends"); return d
def setup_inputs_pairs(rng):
    d = setup_inputs(rng); d["ix"] = lists(rng, "pairs"); return d
def setup_inputs_spread(rng):
    d = setup_inputs(rng); d["wm"] = fit(wide(rng, N, 128, 4 * SH, cols=6)); d["dl"] = fit(wide(rng, N, 128, 4 * R * CH, cols=6)); return d
def check_inputs(d):
    b = []
    for n in ("x", "wm", "dl"):
        v = np.abs(np.asarray(d[n]).astype(np.float32))
        if not np.isfinite(v).all() or ((v > 0) & ((v < 2.0 ** -30) | (v > 2.0 ** 30))).any(): b.append(n)
    for q in range(N):
        e = entries(d["ix"][q])
        if e.min() < 0 or e.max() >= SH or any(len(set(e[CH * t:CH * t + CH].tolist())) != CH for t in range(R)): b.append("ix")
    return b
def reference(x, wm, dl, ix):
    X = [[mx_ref.quantize(np.ascontiguousarray(cut(x[r], t))) for t in range(R + 1)] for r in range(N)]
    y = np.zeros((N, 128, (R + 1) * N * SH), np.float32)
    for q in range(N):
        W = np.array(wm[q]).reshape(128, SH, 4); new = np.array(dl[q]).reshape(128, R * CH, 4); e = entries(ix[q])
        for t in range(R + 1):
            if t: W[:, e[CH * (t - 1):CH * t]] = new[:, CH * (t - 1):CH * t]
            held = mx_ref.quantize(np.array(W).reshape(128, 4 * SH)); k = SH * (t * N + q)
            for r in range(N): y[r][:, k:k + SH] = mx_ref.matmul(X[r][t], held)
    return {"y": y}

@@ -1,0 +1,285 @@
+from concourse.bass import DstId, RemoteDMATransfer
+from concourse.mybir import dt, AluOpType, ActivationFunctionType
+
+N, SH, CH, R = 4, 256, 64, 3
+NEW = R * CH
+HELD = SH + NEW
+SEG = SH + 32
+LOW = -8192.0
+
+SCRATCH = {
+    "wmt": ("sbuf", [128, 4 * SH], "bfloat16"),
+    "dlt": ("sbuf", [128, 4 * NEW], "bfloat16"),
+    "xt": ("sbuf", [128, 512 * (R + 1)], "bfloat16"),
+    "xq": ("sbuf", [128, 512], "float8_e4m3fn_x4"),
+    "xsc": ("sbuf", [128, 512], "uint8"),
+    "lst": ("sbuf", [128, 12], "int32"),
+    "off": ("sbuf", [128, 12], "uint16"),
+    "vals": ("sbuf", [128, NEW], "bfloat16"),
+    "row": ("sbuf", [128, R * SEG], "bfloat16"),
+    "tr": ("sbuf", [128, R * SEG], "bfloat16"),
+    "pi": ("sbuf", [128, 2], "int32"),
+    "up": ("sbuf", [128, SEG], "float32"),
+    "si": ("sbuf", [128, 2], "int32"),
+    "sh": ("sbuf", [128, 2], "float32"),
+    "odd": ("sbuf", [128, 2], "float32"),
+    "even": ("sbuf", [128, 2], "float32"),
+    "pos": ("sbuf", [128, 2], "float32"),
+    "pa": ("sbuf", [128, 54], "float32"),
+    "pb": ("sbuf", [128, 54], "float32"),
+    "gg": ("sbuf", [128, 52], "float32"),
+    "nn": ("sbuf", [128, 16], "float32"),
+    "mt": ("sbuf", [128, 32], "float32"),
+    "tdram": ("dram", [128, 4], "uint16"),
+}
+for _q in range(N):
+    SCRATCH["win%d" % _q] = ("sbuf", [128, HELD], "float8_e4m3fn_x4")
+    SCRATCH["scl%d" % _q] = ("sbuf", [128, HELD], "uint8")
+    SCRATCH["wc%d" % _q] = ("sbuf", [128, R * SH], "float8_e4m3fn_x4")
+    SCRATCH["ws%d" % _q] = ("sbuf", [128, R * SH], "uint8")
+    SCRATCH["tab%d" % _q] = ("sbuf", [128, 48], "uint16")
+    SCRATCH["ld%d" % _q] = ("dram", [128, 4], "uint16")
+for _h in range(2):
+    for _t in range(R + 1):
+        SCRATCH["y%d%d" % (_h, _t)] = ("sbuf", [128, 512], "float32")
+for _b in range(8):
+    SCRATCH["ps%d" % _b] = ("psum", [128, 512], "float32")
+
+SEMAPHORES = ["sv", "ss", "st", "sg", "lix", "lwm", "ldl", "lx0", "lx1", "tdr", "ysem", "ls"]
+for _q in range(N):
+    SEMAPHORES += ["ac%d" % _q, "as%d" % _q, "at%d" % _q, "ad%d" % _q, "tl%d" % _q]
+
+
+def rank_program(g, core, T, topo):
+    r = T.rank_of(core)
+    if r is None:
+        return
+    A = AluOpType
+    COPY = ActivationFunctionType.Copy
+    queues = {"v": g.vector, "s": g.scalar, "t": g.tensor, "g": g, "y": g.sync}
+    count = {}
+    ev = {}
+    seen = {}
+
+    def after(qn, *names):
+        for n in names:
+            sem, val = ev[n]
+            if seen.get((qn, sem), 0) < val:
+                queues[qn].wait_ge(T.sem[sem], val)
+                seen[(qn, sem)] = val
+
+    def did(ins, sem, name, n=1):
+        count[sem] = count.get(sem, 0) + n
+        ins.then_inc(T.sem[sem], n)
+        ev[name] = (sem, count[sem])
+
+    mine = [q for q in range(N) if topo.die(T.cores[q]) == topo.die(core)]
+    other = [q for q in range(N) if q not in mine]
+    near = [q for q in mine if q != r][0]
+    i = mine.index(r)
+    far1, far2 = other[i], other[1 - i]
+    peers = [near, far1, far2]
+    hh, fh = r // 2, far1 // 2
+    for q in peers:
+        ev["codes%d" % q] = ("ac%d" % q, 16)
+        ev["scales%d" % q] = ("as%d" % q, 16)
+        ev["tab%d_1" % q] = ("at%d" % q, 16)
+        for t in (2, 3):
+            ev["tab%d_%d" % (q, t)] = ("at%d" % q, 16) if q == near else ("tl%d" % q, 128)
+        ev["ld%d" % q] = ("ad%d" % q, 16)
+
+    nls = [0]
+
+    def send(src, dst, sem, dsts):
+        ids = []
+        for q in dsts:
+            rid, pid, _ = topo.addr(T.cores[q])
+            ids.append(DstId(rid=rid, pnc=pid))
+        m = topo.mask(core, T.cores[dsts[0]])
+        g.remote_dma_fused([RemoteDMATransfer(dst_ids=ids, dma_engine_mask=m, remote_sem=T.sem[sem], srcs=[src],
+                                              dsts=[dst for _ in dsts])], local_sem=T.sem["ls"])
+        nls[0] += len(topo.engines(core, T.cores[dsts[0]]))
+
+    def send_codes(q, dsts):
+        after("g", "codes%d" % q)
+        w = T["win%d" % q][:].bitcast(dt.uint8)
+        send(w, w, "ac%d" % q, dsts)
+
+    def send_scales(q, dsts):
+        after("g", "scales%d" % q)
+        w = T["scl%d" % q][:]
+        send(w, w, "as%d" % q, dsts)
+
+    win, scl, tab = T["win%d" % r], T["scl%d" % r], T["tab%d" % r]
+    v = g.vector
+
+    for k in range(4):
+        g.sync.dma_start(T.lst[16 * k:16 * k + 16, :], T.ix[:]).then_inc(T.sem["lix"], 16)
+        g.scalar.dma_start(T.lst[64 + 16 * k:80 + 16 * k, :], T.ix[:]).then_inc(T.sem["lix"], 16)
+    ev["ix"] = ("lix", 128)
+    did(g.sync.dma_start(T.wmt[:], T.wm[:]), "lwm", "wm", 16)
+    did(g.sync.dma_start(T.dlt[:], T.dl[:]), "ldl", "dl", 16)
+    did(g.sync.dma_start(T.xt[:, 0:1024], T.x[:, 0:1024]), "lx0", "x0", 16)
+    after("y", "wm")
+    did(g.sync.dma_start(T.xt[:, 1024:2048], T.x[:, 1024:2048]), "lx1", "x1", 16)
+
+    did(g.iota(T.pi[:], [[0, 2]], 0, 1), "sg", "pi")
+    did(g.iota(T.up[:], [[1, SEG]], -SEG, 0, allow_small_or_imprecise_dtypes=True), "sg", "up")
+    did(g.iota(T.vals[:], [[1, NEW]], 0, 0, allow_small_or_imprecise_dtypes=True), "sg", "vals")
+    after("v", "pi")
+    did(v.tensor_scalar(T.si[:], T.pi[:], 4, 1, A.logical_shift_right, A.bitwise_and), "sv", "si")
+    did(v.memset(T.row[:, SEG:R * SEG], LOW), "sv", "low")
+    after("v", "si")
+    did(v.tensor_scalar(T.sh[:], T.si[:], 16, None, A.mult), "sv", "sh")
+    did(v.tensor_scalar(T.pos[:], T.si[:], -16, 32, A.mult, A.add), "sv", "pos")
+    did(v.tensor_copy(T.odd[:], T.si[:]), "sv", "odd")
+    did(v.tensor_scalar(T.even[:], T.si[:], -1, 1, A.mult, A.add), "sv", "even")
+    after("v", "sh", "up")
+    did(v.tensor_scalar(T.row[:, 0:SEG], T.up[:], T.sh[:, 0:1], None, A.add), "sv", "row")
+
+    def qx(h):
+        after("v", "x%d" % h)
+        did(v.quantize_mx(T.xq[:, 256 * h:256 * h + 256], T.xsc[:, 256 * h:256 * h + 256], T.xt[:, 1024 * h:1024 * h + 1024]), "sv", "xq%d" % h)
+
+    def pick(q, t0, t1):
+        a, b = SH * (t0 - 1), SH * t1
+        o = T["tab%d" % q][:, 16 * (t0 - 1):16 * t1]
+        after("v", "codes%d" % q, "tab%d_%d" % (q, t1))
+        did(v.tensor_copy(T["wc%d" % q][:, a:b].bitcast(dt.uint32), T["win%d" % q][:].bitcast(dt.uint32).indirect(o)), "sv", "pc")
+        after("s", "scales%d" % q, "tab%d_%d" % (q, t1))
+        did(g.scalar.activation(T["ws%d" % q][:, a:b], T["scl%d" % q][:].indirect(o), COPY), "ss", "pq")
+        for t in range(t0, t1 + 1):
+            ev["pc%d%d" % (q, t)], ev["pq%d%d" % (q, t)] = ev["pc"], ev["pq"]
+
+    bank = {}
+    last = {}
+
+    def product(t, q):
+        b = len(bank) % 8
+        after("t", "xq%d" % (t // 2))
+        if b in last:
+            after("t", last[b])
+        after("t", *(("codes%d" % q, "scales%d" % q) if t == 0 else ("pc%d%d" % (q, t), "pq%d%d" % (q, t))))
+        w, sc = ("win%d", "scl%d") if t == 0 else ("wc%d", "ws%d")
+        c = SH * max(t - 1, 0)
+        x0 = 128 * t
+        did(g.tensor.matmul_mx(T["ps%d" % b][:, 0:SH], T.xq[:, x0:x0 + 128], T.xsc[:, x0:x0 + 128],
+                               T[w % q][:, c:c + SH], T[sc % q][:, c:c + SH], True, True), "st", "p%d_%d" % (t, q))
+        bank[(t, q)] = b
+        last[b] = "e%d_%d" % (t, q)
+
+    def evac(qn, t, q):
+        c = SH * (q % 2)
+        after(qn, "p%d_%d" % (t, q))
+        out, src = T["y%d%d" % (q // 2, t)][:, c:c + SH], T["ps%d" % bank[(t, q)]][:, 0:SH]
+        if qn == "v":
+            did(v.tensor_copy(out, src), "sv", "e%d_%d" % (t, q))
+        else:
+            did(g.scalar.activation(out, src, COPY), "ss", "e%d_%d" % (t, q))
+
+    def store(t, h):
+        after("y", "e%d_%d" % (t, 2 * h), "e%d_%d" % (t, 2 * h + 1))
+        k = SH * (t * N + 2 * h)
+        did(g.sync.dma_start(T.y[:, k:k + 512], T["y%d%d" % (h, t)][:]), "ysem", "y", 16)
+
+    def repeat(q):
+        after("y", "ld%d" % q)
+        for k in range(8):
+            g.sync.dma_start(T["tab%d" % q][16 * k:16 * k + 16, 16:48], T["ld%d" % q][:]).then_inc(T.sem["tl%d" % q], 16)
+
+    after("v", "ix", "pos")
+    did(v.tensor_scalar(T.off[:], T.lst[:], T.pos[:, 0:1], None, A.add), "sv", "off")
+    after("v", "off", "row", "low", "vals")
+    for t in range(R):
+        did(v.tensor_copy(T.row[:, SEG * t:SEG * t + SEG].indirect(T.off[:, 4 * t:4 * t + 4]), T.vals[:, CH * t:CH * t + CH]), "sv", "scat")
+    after("v", "wm")
+    did(v.quantize_mx(win[:, 0:SH], scl[:, 0:SH], T.wmt[:]), "sv", "base")
+    after("v", "dl")
+    did(v.quantize_mx(win[:, SH:HELD], scl[:, SH:HELD], T.dlt[:]), "sv", "delta")
+    ev["codes%d" % r] = ev["scales%d" % r] = ev["delta"]
+
+    after("v", "scat")
+    did(v.transpose(T.tr[:], T.row[:]), "sv", "tr")
+    qx(0)
+    product(0, r)
+    evac("s", 0, r)
+    after("v", "tr", "odd", "even")
+    did(v.tensor_scalar(T.pa[:], T.tr[:, 0:R * SEG:16], T.even[:, 0:1], None, A.mult), "sv", "pa")
+    did(v.tensor_scalar(T.pb[:], T.tr[:, 0:R * SEG:16], T.odd[:, 0:1], None, A.mult), "sv", "pb")
+    after("v", "pa", "pb")
+    did(v.tensor_tensor(T.gg[:], T.pa[:, 2:54], T.pb[:, 1:53], A.add), "sv", "gg")
+    after("v", "gg")
+    did(v.tensor_tensor(T.mt[:, 0:16], T.gg[:, 0:16], T.gg[:, 18:34], A.max), "sv", "m2")
+    did(v.tensor_tensor(T.nn[:], T.gg[:, 18:34], T.gg[:, 36:52], A.max), "sv", "nn")
+    did(v.tensor_scalar(tab[:, 0:16], T.gg[:, 0:16], SH, None, A.add), "sv", "tab1")
+    after("v", "nn")
+    did(v.tensor_tensor(T.mt[:, 16:32], T.nn[:], T.gg[:, 0:16], A.max), "sv", "m3")
+    after("v", "m3")
+    did(v.tensor_scalar(tab[:, 16:48], T.mt[:], SH, None, A.add), "sv", "tab")
+    for t in (1, 2, 3):
+        ev["tab%d_%d" % (r, t)] = ev["tab"]
+
+    send_scales(r, [far1])
+    send_scales(r, [near])
+    send_codes(r, [near])
+    after("y", "tab")
+    did(g.sync.dma_start(T.tdram[:], tab[0:16, 16:48]), "tdr", "tdram", 16)
+    after("g", "tab")
+    send(tab[:], tab[:], "at%d" % r, [near])
+    send_codes(r, [far1])
+    send(tab[:, 0:16], tab[:, 0:16], "at%d" % r, [far1, far2])
+    after("g", "tdram")
+    send(T.tdram[:], T["ld%d" % r][:], "ad%d" % r, [far1, far2])
+    send_scales(far1, [near])
+    send_codes(far1, [near])
+
+    qx(1)
+    pick(r, 1, 3)
+    product(0, near)
+    evac("v", 0, near)
+    store(0, hh)
+    for t in (1, 2, 3):
+        product(t, r)
+    pick(near, 1, 2)
+    pick(near, 3, 3)
+    evac("v", 1, r)
+    evac("v", 2, r)
+    for t in (1, 2, 3):
+        product(t, near)
+    evac("s", 3, r)
+    repeat(far1)
+    repeat(far2)
+    pick(far1, 1, 1)
+    evac("s", 1, near)
+    evac("v", 2, near)
+    store(1, hh)
+    store(2, hh)
+    product(0, far1)
+    product(0, far2)
+    evac("s", 3, near)
+    store(3, hh)
+    pick(far2, 1, 1)
+    evac("s", 0, far1)
+    evac("v", 0, far2)
+    store(0, fh)
+    product(1, far1)
+    product(1, far2)
+    pick(far1, 2, 3)
+    pick(far2, 2, 2)
+    evac("v", 1, far1)
+    evac("s", 1, far2)
+    store(1, fh)
+    product(2, far1)
+    product(3, far1)
+    pick(far2, 3, 3)
+    product(2, far2)
+    evac("v", 2, far1)
+    product(3, far2)
+    evac("s", 2, far2)
+    store(2, fh)
+    evac("v", 3, far1)
+    evac("s", 3, far2)
+    store(3, fh)
+
+    g.wait_ge(T.sem["ls"], nls[0])
+    after("y", "y")

@@ -6,6 +6,7 @@ NEW = R * CH
 HELD = SH + NEW
 SEG = SH + 32
 LOW = -8192.0
+HALF = 24
 
 SCRATCH = {
     "wmt": ("sbuf", [128, 4 * SH], "bfloat16"),
@@ -13,41 +14,48 @@ SCRATCH = {
     "xt": ("sbuf", [128, 512 * (R + 1)], "bfloat16"),
     "xq": ("sbuf", [128, 512], "float8_e4m3fn_x4"),
     "xsc": ("sbuf", [128, 512], "uint8"),
-    "lst": ("sbuf", [128, 12], "int32"),
-    "off": ("sbuf", [128, 12], "uint16"),
-    "vals": ("sbuf", [128, NEW], "bfloat16"),
-    "row": ("sbuf", [128, R * SEG], "bfloat16"),
-    "tr": ("sbuf", [128, R * SEG], "bfloat16"),
+    "lst": ("sbuf", [128, 24], "int32"),
+    "off": ("sbuf", [128, 16], "uint16"),
+    "vals": ("sbuf", [128, CH], "bfloat16"),
+    "row": ("sbuf", [128, SEG], "bfloat16"),
+    "tr": ("sbuf", [128, SEG], "bfloat16"),
     "pi": ("sbuf", [128, 2], "int32"),
-    "up": ("sbuf", [128, SEG], "float32"),
+    "kk": ("sbuf", [128, CH], "float32"),
+    "c16": ("sbuf", [128, 16], "float32"),
+    "same": ("sbuf", [128, 16], "float32"),
     "si": ("sbuf", [128, 2], "int32"),
-    "sh": ("sbuf", [128, 2], "float32"),
-    "odd": ("sbuf", [128, 2], "float32"),
-    "even": ("sbuf", [128, 2], "float32"),
-    "pos": ("sbuf", [128, 2], "float32"),
-    "pa": ("sbuf", [128, 54], "float32"),
-    "pb": ("sbuf", [128, 54], "float32"),
-    "gg": ("sbuf", [128, 52], "float32"),
-    "nn": ("sbuf", [128, 16], "float32"),
-    "mt": ("sbuf", [128, 32], "float32"),
-    "tdram": ("dram", [128, 4], "uint16"),
+    "qa": ("sbuf", [128, 2], "int32"),
+    "lo": ("sbuf", [128, 2], "int32"),
+    "lof": ("sbuf", [128, 2], "float32"),
+    "npos": ("sbuf", [128, 2], "float32"),
+    "a4": ("sbuf", [128, 2], "float32"),
+    "a64": ("sbuf", [128, 2], "float32"),
+    "sel0": ("sbuf", [128, 2], "uint16"),
+    "selt": ("sbuf", [128, 2], "uint16"),
+    "pp": ("sbuf", [128, 48], "float32"),
+    "tab": ("sbuf", [128, 48], "uint16"),
+    "half": ("sbuf", [128, HALF], "bfloat16"),
+    "hl": ("sbuf", [128, 2 * HALF], "bfloat16"),
+    "tn": ("sbuf", [128, 32], "uint16"),
+    "tb": ("sbuf", [128, 4 * HALF], "uint16"),
+    "fw": ("sbuf", [128, 4], "int32"),
+    "fwo": ("sbuf", [128, 4], "uint16"),
+    "new1": ("sbuf", [128, CH], "float32"),
 }
 for _q in range(N):
     SCRATCH["win%d" % _q] = ("sbuf", [128, HELD], "float8_e4m3fn_x4")
     SCRATCH["scl%d" % _q] = ("sbuf", [128, HELD], "uint8")
     SCRATCH["wc%d" % _q] = ("sbuf", [128, R * SH], "float8_e4m3fn_x4")
     SCRATCH["ws%d" % _q] = ("sbuf", [128, R * SH], "uint8")
-    SCRATCH["tab%d" % _q] = ("sbuf", [128, 48], "uint16")
-    SCRATCH["ld%d" % _q] = ("dram", [128, 4], "uint16")
 for _h in range(2):
     for _t in range(R + 1):
         SCRATCH["y%d%d" % (_h, _t)] = ("sbuf", [128, 512], "float32")
 for _b in range(8):
     SCRATCH["ps%d" % _b] = ("psum", [128, 512], "float32")
 
-SEMAPHORES = ["sv", "ss", "st", "sg", "lix", "lwm", "ldl", "lx0", "lx1", "tdr", "ysem", "ls"]
+SEMAPHORES = ["sv", "ss", "st", "sg", "lix", "lwm", "ldl", "lx0", "lx1", "ysem", "ls", "afw", "ah", "atn"]
 for _q in range(N):
-    SEMAPHORES += ["ac%d" % _q, "as%d" % _q, "at%d" % _q, "ad%d" % _q, "tl%d" % _q]
+    SEMAPHORES += ["ac%d" % _q, "as%d" % _q]
 
 
 def rank_program(g, core, T, topo):
@@ -56,6 +64,7 @@ def rank_program(g, core, T, topo):
         return
     A = AluOpType
     COPY = ActivationFunctionType.Copy
+    IDENT = ActivationFunctionType.Identity
     queues = {"v": g.vector, "s": g.scalar, "t": g.tensor, "g": g, "y": g.sync}
     count = {}
     ev = {}
@@ -80,75 +89,86 @@ def rank_program(g, core, T, topo):
     far1, far2 = other[i], other[1 - i]
     peers = [near, far1, far2]
     hh, fh = r // 2, far1 // 2
+    eng = topo.engines(core, T.cores[near])
+    every = len(eng)
     for q in peers:
-        ev["codes%d" % q] = ("ac%d" % q, 16)
-        ev["scales%d" % q] = ("as%d" % q, 16)
-        ev["tab%d_1" % q] = ("at%d" % q, 16)
-        for t in (2, 3):
-            ev["tab%d_%d" % (q, t)] = ("at%d" % q, 16) if q == near else ("tl%d" % q, 128)
-        ev["ld%d" % q] = ("ad%d" % q, 16)
+        ev["codes%d" % q] = ("ac%d" % q, every)
+        ev["scales%d" % q] = ("as%d" % q, every)
+    ev["fw"] = ("afw", every)
+    ev["tn"] = ("atn", every)
+    ev["hl"] = ("ah", 2 * every)
 
     nls = [0]
 
-    def send(src, dst, sem, dsts):
+    def send(src, dsts, sem, ranks):
         ids = []
-        for q in dsts:
+        for q in ranks:
             rid, pid, _ = topo.addr(T.cores[q])
             ids.append(DstId(rid=rid, pnc=pid))
-        m = topo.mask(core, T.cores[dsts[0]])
-        g.remote_dma_fused([RemoteDMATransfer(dst_ids=ids, dma_engine_mask=m, remote_sem=T.sem[sem], srcs=[src],
-                                              dsts=[dst for _ in dsts])], local_sem=T.sem["ls"])
-        nls[0] += len(topo.engines(core, T.cores[dsts[0]]))
+        nls[0] += every
+        g.remote_dma_fused([RemoteDMATransfer(dst_ids=ids, dma_engine_mask=topo.mask(core, T.cores[ranks[0]]), remote_sem=T.sem[sem],
+                                              srcs=[src], dsts=dsts)], local_sem=T.sem["ls"])
 
-    def send_codes(q, dsts):
-        after("g", "codes%d" % q)
-        w = T["win%d" % q][:].bitcast(dt.uint8)
-        send(w, w, "ac%d" % q, dsts)
-
-    def send_scales(q, dsts):
-        after("g", "scales%d" % q)
-        w = T["scl%d" % q][:]
-        send(w, w, "as%d" % q, dsts)
-
-    win, scl, tab = T["win%d" % r], T["scl%d" % r], T["tab%d" % r]
+    win, scl = T["win%d" % r], T["scl%d" % r]
     v = g.vector
 
     for k in range(4):
-        g.sync.dma_start(T.lst[16 * k:16 * k + 16, :], T.ix[:]).then_inc(T.sem["lix"], 16)
-        g.scalar.dma_start(T.lst[64 + 16 * k:80 + 16 * k, :], T.ix[:]).then_inc(T.sem["lix"], 16)
+        g.sync.dma_start(T.lst[16 * k:16 * k + 16, 0:12], T.ix[:]).then_inc(T.sem["lix"], 16)
+        g.scalar.dma_start(T.lst[64 + 16 * k:80 + 16 * k, 0:12], T.ix[:]).then_inc(T.sem["lix"], 16)
     ev["ix"] = ("lix", 128)
     did(g.sync.dma_start(T.wmt[:], T.wm[:]), "lwm", "wm", 16)
     did(g.sync.dma_start(T.dlt[:], T.dl[:]), "ldl", "dl", 16)
-    did(g.sync.dma_start(T.xt[:, 0:1024], T.x[:, 0:1024]), "lx0", "x0", 16)
-    after("y", "wm")
-    did(g.sync.dma_start(T.xt[:, 1024:2048], T.x[:, 1024:2048]), "lx1", "x1", 16)
+    did(g.sync.dma_start(T.xt[:, 0:512], T.x[:, 0:512]), "lx0", "x0", 16)
+    did(g.sync.dma_start(T.xt[:, 512:2048], T.x[:, 512:2048]), "lx1", "x1", 16)
 
     did(g.iota(T.pi[:], [[0, 2]], 0, 1), "sg", "pi")
-    did(g.iota(T.up[:], [[1, SEG]], -SEG, 0, allow_small_or_imprecise_dtypes=True), "sg", "up")
-    did(g.iota(T.vals[:], [[1, NEW]], 0, 0, allow_small_or_imprecise_dtypes=True), "sg", "vals")
+    did(g.iota(T.kk[:], [[1, CH]], 0, 0, allow_small_or_imprecise_dtypes=True), "sg", "kk")
+    did(g.iota(T.c16[:], [[16, 16]], -SH, 0, allow_small_or_imprecise_dtypes=True), "sg", "c16")
+    did(v.memset(T.row[:], LOW), "sv", "row")
+    did(v.memset(T.lst[:, 12:24], 0), "sv", "pad")
     after("v", "pi")
+    did(v.tensor_scalar(T.qa[:], T.pi[:], 5, None, A.logical_shift_right), "sv", "qa")
     did(v.tensor_scalar(T.si[:], T.pi[:], 4, 1, A.logical_shift_right, A.bitwise_and), "sv", "si")
-    did(v.memset(T.row[:, SEG:R * SEG], LOW), "sv", "low")
+    did(v.tensor_scalar(T.lo[:], T.pi[:], 15, None, A.bitwise_and), "sv", "lo")
+    after("v", "qa")
+    did(v.tensor_scalar(T.a64[:], T.qa[:], CH, 2 * CH, A.mult, A.min), "sv", "a64")
+    did(v.tensor_scalar(T.a4[:], T.qa[:], 4, 8, A.mult, A.min), "sv", "a4")
     after("v", "si")
-    did(v.tensor_scalar(T.sh[:], T.si[:], 16, None, A.mult), "sv", "sh")
-    did(v.tensor_scalar(T.pos[:], T.si[:], -16, 32, A.mult, A.add), "sv", "pos")
-    did(v.tensor_copy(T.odd[:], T.si[:]), "sv", "odd")
-    did(v.tensor_scalar(T.even[:], T.si[:], -1, 1, A.mult, A.add), "sv", "even")
-    after("v", "sh", "up")
-    did(v.tensor_scalar(T.row[:, 0:SEG], T.up[:], T.sh[:, 0:1], None, A.add), "sv", "row")
+    did(v.tensor_scalar(T.npos[:], T.si[:], 16, -32, A.mult, A.add), "sv", "npos")
+    after("v", "lo")
+    did(v.tensor_copy(T.lof[:], T.lo[:]), "sv", "lof")
+    after("v", "a4")
+    did(v.tensor_scalar(T.sel0[:], T.lo[:], T.a4[:, 0:1], None, A.add), "sv", "sel0")
+    after("v", "npos")
+    did(v.tensor_scalar(T.selt[:], T.lo[:], 16, T.npos[:, 0:1], A.mult, A.subtract), "sv", "selt")
+    after("s", "kk", "a64")
+    did(g.scalar.activation(T.vals[:], T.kk[:], IDENT, bias=T.a64[:, 0:1]), "ss", "vals")
+    after("s", "c16", "lof")
+    did(g.scalar.activation(T.same[:], T.c16[:], IDENT, bias=T.lof[:, 0:1]), "ss", "same")
 
-    def qx(h):
-        after("v", "x%d" % h)
-        did(v.quantize_mx(T.xq[:, 256 * h:256 * h + 256], T.xsc[:, 256 * h:256 * h + 256], T.xt[:, 1024 * h:1024 * h + 1024]), "sv", "xq%d" % h)
-
-    def pick(q, t0, t1):
-        a, b = SH * (t0 - 1), SH * t1
-        o = T["tab%d" % q][:, 16 * (t0 - 1):16 * t1]
-        after("v", "codes%d" % q, "tab%d_%d" % (q, t1))
-        did(v.tensor_copy(T["wc%d" % q][:, a:b].bitcast(dt.uint32), T["win%d" % q][:].bitcast(dt.uint32).indirect(o)), "sv", "pc")
-        after("s", "scales%d" % q, "tab%d_%d" % (q, t1))
-        did(g.scalar.activation(T["ws%d" % q][:, a:b], T["scl%d" % q][:].indirect(o), COPY), "ss", "pq")
+    def qx(t0, t1=None):
+        t1 = t0 if t1 is None else t1
+        after("v", "x%d" % min(t1, 1))
+        a, b = 128 * t0, 128 * t1 + 128
+        did(v.quantize_mx(T.xq[:, a:b], T.xsc[:, a:b], T.xt[:, 4 * a:4 * b]), "sv", "xq")
         for t in range(t0, t1 + 1):
+            ev["xq%d" % t] = ev["xq"]
+
+    def table(q, a, b):
+        if q == r:
+            return T.tab[:, a:b], "tab"
+        if q == near:
+            return T.tn[:, a - 16:b - 16], "tn"
+        c = HALF * (peers.index(q) - 1) + (HALF if a >= HALF else 0)
+        return T.tb[:, c + a:c + b], "tb%d" % (a // HALF)
+
+    def pick(q, a, b):
+        o, e = table(q, a, b)
+        after("v", "codes%d" % q, e)
+        did(v.tensor_copy(T["wc%d" % q][:, 16 * a:16 * b].bitcast(dt.uint32), T["win%d" % q][:].bitcast(dt.uint32).indirect(o)), "sv", "pc")
+        after("s", "scales%d" % q, e)
+        did(g.scalar.activation(T["ws%d" % q][:, 16 * a:16 * b], T["scl%d" % q][:].indirect(o), COPY), "ss", "pq")
+        for t in range(a // 16 + 1, (b - 1) // 16 + 2):
             ev["pc%d%d" % (q, t)], ev["pq%d%d" % (q, t)] = ev["pc"], ev["pq"]
 
     bank = {}
@@ -156,130 +176,153 @@ def rank_program(g, core, T, topo):
 
     def product(t, q):
         b = len(bank) % 8
-        after("t", "xq%d" % (t // 2))
+        after("t", "xq%d" % t)
         if b in last:
             after("t", last[b])
-        after("t", *(("codes%d" % q, "scales%d" % q) if t == 0 else ("pc%d%d" % (q, t), "pq%d%d" % (q, t))))
-        w, sc = ("win%d", "scl%d") if t == 0 else ("wc%d", "ws%d")
-        c = SH * max(t - 1, 0)
+        plain = t == 0 or (t, q) == (1, near)
+        after("t", *(("codes%d" % q, "scales%d" % q) if plain else ("pc%d%d" % (q, t), "pq%d%d" % (q, t))))
+        w, sc = ("win%d", "scl%d") if plain else ("wc%d", "ws%d")
+        c = 0 if plain else SH * (t - 1)
+        n = SH + CH if plain and t else SH
         x0 = 128 * t
-        did(g.tensor.matmul_mx(T["ps%d" % b][:, 0:SH], T.xq[:, x0:x0 + 128], T.xsc[:, x0:x0 + 128],
-                               T[w % q][:, c:c + SH], T[sc % q][:, c:c + SH], True, True), "st", "p%d_%d" % (t, q))
+        did(g.tensor.matmul_mx(T["ps%d" % b][:, 0:n], T.xq[:, x0:x0 + 128], T.xsc[:, x0:x0 + 128],
+                               T[w % q][:, c:c + n], T[sc % q][:, c:c + n], True, True), "st", "p%d_%d" % (t, q))
         bank[(t, q)] = b
         last[b] = "e%d_%d" % (t, q)
+
+    def copy_out(qn, out, src, name):
+        if qn == "v":
+            did(v.tensor_copy(out, src), "sv", name)
+        else:
+            did(g.scalar.activation(out, src, COPY), "ss", name)
 
     def evac(qn, t, q):
         c = SH * (q % 2)
         after(qn, "p%d_%d" % (t, q))
-        out, src = T["y%d%d" % (q // 2, t)][:, c:c + SH], T["ps%d" % bank[(t, q)]][:, 0:SH]
-        if qn == "v":
-            did(v.tensor_copy(out, src), "sv", "e%d_%d" % (t, q))
-        else:
-            did(g.scalar.activation(out, src, COPY), "ss", "e%d_%d" % (t, q))
+        ps = T["ps%d" % bank[(t, q)]]
+        if (t, q) == (1, near):
+            copy_out(qn, T.new1[:], ps[:, SH:SH + CH], "new1")
+        copy_out(qn, T["y%d%d" % (q // 2, t)][:, c:c + SH], ps[:, 0:SH], "e%d_%d" % (t, q))
+        ev["b%d_%d" % (t, q)] = ev["e%d_%d" % (t, q)]
 
-    def store(t, h):
-        after("y", "e%d_%d" % (t, 2 * h), "e%d_%d" % (t, 2 * h + 1))
+    def replace():
+        c = SH * (near % 2)
+        after("v", "fwo", "new1", "e1_%d" % near)
+        did(v.tensor_copy(T["y%d1" % hh][:, c:c + SH].indirect(T.fwo[:]), T.new1[:]), "sv", "b1_%d" % near)
+
+    def store(t, h, qn="y"):
+        after(qn, "b%d_%d" % (t, 2 * h), "b%d_%d" % (t, 2 * h + 1))
         k = SH * (t * N + 2 * h)
-        did(g.sync.dma_start(T.y[:, k:k + 512], T["y%d%d" % (h, t)][:]), "ysem", "y", 16)
+        did(queues[qn].dma_start(T.y[:, k:k + 512], T["y%d%d" % (h, t)][:]), "ysem", "y", 16)
 
-    def repeat(q):
-        after("y", "ld%d" % q)
-        for k in range(8):
-            g.sync.dma_start(T["tab%d" % q][16 * k:16 * k + 16, 16:48], T["ld%d" % q][:]).then_inc(T.sem["tl%d" % q], 16)
+    def store1(t, q, qn="y"):
+        after(qn, "b%d_%d" % (t, q))
+        k, c = SH * (t * N + q), SH * (q % 2)
+        did(queues[qn].dma_start(T.y[:, k:k + SH], T["y%d%d" % (q // 2, t)][:, c:c + SH]), "ysem", "y", 16)
 
-    after("v", "ix", "pos")
-    did(v.tensor_scalar(T.off[:], T.lst[:], T.pos[:, 0:1], None, A.add), "sv", "off")
-    after("v", "off", "row", "low", "vals")
-    for t in range(R):
-        did(v.tensor_copy(T.row[:, SEG * t:SEG * t + SEG].indirect(T.off[:, 4 * t:4 * t + 4]), T.vals[:, CH * t:CH * t + CH]), "sv", "scat")
+    def out(qn, t, q):
+        evac(qn, t, q)
+        store1(t, q)
+
+    def spread(k):
+        after("v", "hl")
+        for a in (0, 64):
+            did(v.tensor_scalar(T.tb[a:a + 64, 2 * HALF * k:2 * HALF * (k + 1)], T.hl[64 * k:64 * k + 64, :], SH, None, A.add), "sv", "tb%d" % k)
+
+    after("g", "ix")
+    send(T.lst[:, 0:4], [T.fw[:]], "afw", [near])
+
+    after("v", "ix", "pad", "sel0", "npos")
+    did(v.tensor_scalar(T.off[:], T.lst[:].indirect(T.sel0[:, 0:1]), T.npos[:, 0:1], None, A.subtract), "sv", "off")
+    after("v", "off", "row", "vals")
+    did(v.tensor_copy(T.row[:].indirect(T.off[:, 0:4]), T.vals[:]), "sv", "scat")
     after("v", "wm")
     did(v.quantize_mx(win[:, 0:SH], scl[:, 0:SH], T.wmt[:]), "sv", "base")
+    after("v", "scat")
+    did(v.transpose(T.tr[:], T.row[:]), "sv", "tr")
     after("v", "dl")
     did(v.quantize_mx(win[:, SH:HELD], scl[:, SH:HELD], T.dlt[:]), "sv", "delta")
     ev["codes%d" % r] = ev["scales%d" % r] = ev["delta"]
-
-    after("v", "scat")
-    did(v.transpose(T.tr[:], T.row[:]), "sv", "tr")
+    after("v", "tr", "selt", "same")
+    did(v.tensor_tensor(T.pp[:, 0:16], T.tr[:].indirect(T.selt[:, 0:1]), T.same[:], A.max), "sv", "q")
     qx(0)
     product(0, r)
-    evac("s", 0, r)
-    after("v", "tr", "odd", "even")
-    did(v.tensor_scalar(T.pa[:], T.tr[:, 0:R * SEG:16], T.even[:, 0:1], None, A.mult), "sv", "pa")
-    did(v.tensor_scalar(T.pb[:], T.tr[:, 0:R * SEG:16], T.odd[:, 0:1], None, A.mult), "sv", "pb")
-    after("v", "pa", "pb")
-    did(v.tensor_tensor(T.gg[:], T.pa[:, 2:54], T.pb[:, 1:53], A.add), "sv", "gg")
-    after("v", "gg")
-    did(v.tensor_tensor(T.mt[:, 0:16], T.gg[:, 0:16], T.gg[:, 18:34], A.max), "sv", "m2")
-    did(v.tensor_tensor(T.nn[:], T.gg[:, 18:34], T.gg[:, 36:52], A.max), "sv", "nn")
-    did(v.tensor_scalar(tab[:, 0:16], T.gg[:, 0:16], SH, None, A.add), "sv", "tab1")
-    after("v", "nn")
-    did(v.tensor_tensor(T.mt[:, 16:32], T.nn[:], T.gg[:, 0:16], A.max), "sv", "m3")
+    after("v", "q")
+    did(v.tensor_tensor(T.pp[0:32, 16:32], T.pp[0:32, 0:16], T.pp[32:64, 0:16], A.max), "sv", "m2")
+    after("v", "m2")
+    did(v.tensor_tensor(T.pp[0:32, 32:48], T.pp[0:32, 16:32], T.pp[64:96, 0:16], A.max), "sv", "m3")
     after("v", "m3")
-    did(v.tensor_scalar(tab[:, 16:48], T.mt[:], SH, None, A.add), "sv", "tab")
-    for t in (1, 2, 3):
-        ev["tab%d_%d" % (r, t)] = ev["tab"]
+    for a in range(0, 128, 32):
+        did(v.tensor_scalar(T.tab[a:a + 32, :], T.pp[0:32, :], SH, None, A.add), "sv", "tab")
 
-    send_scales(r, [far1])
-    send_scales(r, [near])
-    send_codes(r, [near])
-    after("y", "tab")
-    did(g.sync.dma_start(T.tdram[:], tab[0:16, 16:48]), "tdr", "tdram", 16)
-    after("g", "tab")
-    send(tab[:], tab[:], "at%d" % r, [near])
-    send_codes(r, [far1])
-    send(tab[:, 0:16], tab[:, 0:16], "at%d" % r, [far1, far2])
-    after("g", "tdram")
-    send(T.tdram[:], T["ld%d" % r][:], "ad%d" % r, [far1, far2])
-    send_scales(far1, [near])
-    send_codes(far1, [near])
+    def halves():
+        for a in range(0, 128, 32):
+            c = HALF * (a // 64)
+            after("s", "m3")
+            did(g.scalar.activation(T.half[a:a + 32, :], T.pp[0:32, c:c + HALF], COPY), "ss", "half")
 
+    halves()
+    evac("s", 0, r)
     qx(1)
-    pick(r, 1, 3)
+    pick(r, 0, 16)
+
+    codes = win[:].bitcast(dt.uint8)
+    after("g", "delta")
+    send(codes, [codes], "ac%d" % r, [near])
+    send(scl[:], [scl[:]] * 3, "as%d" % r, peers)
+    after("g", "half")
+    send(T.half[:], [T.hl[:, 0:HALF], T.hl[:, HALF:2 * HALF]], "ah", [far1, far2])
+    after("g", "tab")
+    send(T.tab[:, 16:48], [T.tn[:]], "atn", [near])
+    send(codes, [codes], "ac%d" % r, [far1])
+    send(codes, [codes], "ac%d" % r, [far2])
+
+    product(1, r)
+    qx(2, 3)
+    pick(r, 16, 32)
+    product(2, r)
+    pick(r, 32, 48)
+    product(3, r)
+    after("v", "fw")
+    did(v.tensor_copy(T.fwo[:], T.fw[:]), "sv", "fwo")
+    out("v", 1, r)
+    store1(0, r)
+    out("s", 2, r)
     product(0, near)
-    evac("v", 0, near)
-    store(0, hh)
-    for t in (1, 2, 3):
-        product(t, r)
-    pick(near, 1, 2)
-    pick(near, 3, 3)
-    evac("v", 1, r)
-    evac("v", 2, r)
-    for t in (1, 2, 3):
-        product(t, near)
-    evac("s", 3, r)
-    repeat(far1)
-    repeat(far2)
-    pick(far1, 1, 1)
+    product(1, near)
+    pick(near, 16, 48)
+    out("v", 3, r)
     evac("s", 1, near)
-    evac("v", 2, near)
-    store(1, hh)
-    store(2, hh)
+    out("s", 0, near)
+    product(2, near)
+    product(3, near)
+    spread(0)
+    pick(far1, 0, 24)
+    replace()
+    store1(1, near)
+    out("v", 2, near)
+    out("s", 3, near)
     product(0, far1)
-    product(0, far2)
-    evac("s", 3, near)
-    store(3, hh)
-    pick(far2, 1, 1)
-    evac("s", 0, far1)
-    evac("v", 0, far2)
-    store(0, fh)
     product(1, far1)
+    spread(1)
+    pick(far2, 0, 24)
+    product(0, far2)
     product(1, far2)
-    pick(far1, 2, 3)
-    pick(far2, 2, 2)
-    evac("v", 1, far1)
-    evac("s", 1, far2)
-    store(1, fh)
+    out("s", 0, far1)
+    out("v", 1, far1)
+    pick(far1, 24, 48)
     product(2, far1)
     product(3, far1)
-    pick(far2, 3, 3)
+    out("s", 0, far2)
+    out("s", 1, far2)
+    pick(far2, 24, 32)
     product(2, far2)
-    evac("v", 2, far1)
+    pick(far2, 32, 48)
     product(3, far2)
-    evac("s", 2, far2)
-    store(2, fh)
-    evac("v", 3, far1)
-    evac("s", 3, far2)
-    store(3, fh)
+    out("v", 2, far1)
+    out("v", 3, far1)
+    out("s", 2, far2)
+    out("v", 3, far2)
 
     g.wait_ge(T.sem["ls"], nls[0])
     after("y", "y")

@@ -6,7 +6,7 @@ NEW = R * CH
 HELD = SH + NEW
 SEG = SH + 32
 LOW = -8192.0
-HALF = 24
+XPARTS = [(0, 1), (1, 2), (2, 4)]
 
 SCRATCH = {
     "wmt": ("sbuf", [128, 4 * SH], "bfloat16"),
@@ -14,8 +14,9 @@ SCRATCH = {
     "xt": ("sbuf", [128, 512 * (R + 1)], "bfloat16"),
     "xq": ("sbuf", [128, 512], "float8_e4m3fn_x4"),
     "xsc": ("sbuf", [128, 512], "uint8"),
-    "lst": ("sbuf", [128, 24], "int32"),
-    "off": ("sbuf", [128, 16], "uint16"),
+    "lst": ("sbuf", [128, 12], "int32"),
+    "idle": ("sbuf", [128, 4], "int32"),
+    "off": ("sbuf", [128, 4], "uint16"),
     "vals": ("sbuf", [128, CH], "bfloat16"),
     "row": ("sbuf", [128, SEG], "bfloat16"),
     "tr": ("sbuf", [128, SEG], "bfloat16"),
@@ -28,39 +29,70 @@ SCRATCH = {
     "lo": ("sbuf", [128, 2], "int32"),
     "lof": ("sbuf", [128, 2], "float32"),
     "npos": ("sbuf", [128, 2], "float32"),
-    "a4": ("sbuf", [128, 2], "float32"),
     "a64": ("sbuf", [128, 2], "float32"),
-    "sel0": ("sbuf", [128, 2], "uint16"),
     "selt": ("sbuf", [128, 2], "uint16"),
     "pp": ("sbuf", [128, 48], "float32"),
     "tab": ("sbuf", [128, 48], "uint16"),
-    "half": ("sbuf", [128, HALF], "bfloat16"),
-    "hl": ("sbuf", [128, 2 * HALF], "bfloat16"),
     "tn": ("sbuf", [128, 32], "uint16"),
-    "tb": ("sbuf", [128, 4 * HALF], "uint16"),
-    "fw": ("sbuf", [128, 4], "int32"),
+    "t1": ("sbuf", [128, 48], "uint16"),
+    "t2": ("sbuf", [128, 48], "uint16"),
+    "td": ("dram", [128, 6], "uint16"),
+    "ld": ("dram", [128, 6], "uint16"),
     "fwo": ("sbuf", [128, 4], "uint16"),
-    "new1": ("sbuf", [128, CH], "float32"),
+    "fw": ("sbuf", [128, 4], "uint16"),
 }
 for _q in range(N):
     SCRATCH["win%d" % _q] = ("sbuf", [128, HELD], "float8_e4m3fn_x4")
     SCRATCH["scl%d" % _q] = ("sbuf", [128, HELD], "uint8")
     SCRATCH["wc%d" % _q] = ("sbuf", [128, R * SH], "float8_e4m3fn_x4")
     SCRATCH["ws%d" % _q] = ("sbuf", [128, R * SH], "uint8")
-for _h in range(2):
     for _t in range(R + 1):
-        SCRATCH["y%d%d" % (_h, _t)] = ("sbuf", [128, 512], "float32")
+        SCRATCH["y%d%d" % (_t, _q)] = ("sbuf", [128, SH + CH * (_t == 1)], "float32")
 for _b in range(8):
     SCRATCH["ps%d" % _b] = ("psum", [128, 512], "float32")
 
-SEMAPHORES = ["sv", "ss", "st", "sg", "lix", "lwm", "ldl", "lx0", "lx1", "ysem", "ls", "afw", "ah", "atn"]
+SEMAPHORES = ["sv", "ss", "st", "sg", "lix", "lwm", "ldl", "lx0", "lx1", "lx2", "ltd", "lt2", "ysem", "ls", "afw", "atn", "at1", "ald"]
 for _q in range(N):
     SEMAPHORES += ["ac%d" % _q, "as%d" % _q]
+
+
+def places(q, T, topo):
+    die = topo.die(T.cores[q])
+    mine = [p for p in range(N) if topo.die(T.cores[p]) == die]
+    other = [p for p in range(N) if p not in mine]
+    spare = [c for c in topo.cores_of(T.cores[q]) if T.rank_of(c) is None and topo.die(c) != die]
+    i = mine.index(q)
+    return mine[1 - i], other[i], other[1 - i], spare[i]
+
+
+def write(g, core, T, topo, src, dst, sem, cores):
+    ids = []
+    for c in cores:
+        rid, pid, _ = topo.addr(c)
+        ids.append(DstId(rid=rid, pnc=pid))
+    g.remote_dma_fused([RemoteDMATransfer(dst_ids=ids, dma_engine_mask=topo.mask(core, cores[0]), remote_sem=T.sem[sem],
+                                          srcs=[src], dsts=[dst for _ in cores])], local_sem=T.sem["ls"])
+    return len(topo.engines(core, cores[0]))
+
+
+def hand_on(g, core, T, topo):
+    for q in range(N):
+        _, far1, far2, spare = places(q, T, topo)
+        if spare == core and HELP:
+            sent = 0
+            for sem, w in (("as%d" % q, T["scl%d" % q][:]), ("ac%d" % q, T["win%d" % q][:].bitcast(dt.uint8))):
+                g.wait_ge(T.sem[sem], len(topo.engines(T.cores[q], core)))
+                sent += write(g, core, T, topo, w, w, sem, [T.cores[far1], T.cores[far2]])
+            g.wait_ge(T.sem["ls"], sent)
+
+
+HELP = False
 
 
 def rank_program(g, core, T, topo):
     r = T.rank_of(core)
     if r is None:
+        hand_on(g, core, T, topo)
         return
     A = AluOpType
     COPY = ActivationFunctionType.Copy
@@ -82,247 +114,225 @@ def rank_program(g, core, T, topo):
         ins.then_inc(T.sem[sem], n)
         ev[name] = (sem, count[sem])
 
-    mine = [q for q in range(N) if topo.die(T.cores[q]) == topo.die(core)]
-    other = [q for q in range(N) if q not in mine]
-    near = [q for q in mine if q != r][0]
-    i = mine.index(r)
-    far1, far2 = other[i], other[1 - i]
-    peers = [near, far1, far2]
-    hh, fh = r // 2, far1 // 2
-    eng = topo.engines(core, T.cores[near])
-    every = len(eng)
-    for q in peers:
+    near, far1, far2, spare = places(r, T, topo)
+    cores = list(T.cores) + [spare]
+    H = N
+    every = len(topo.engines(core, T.cores[near]))
+    for q in (near, far1, far2):
         ev["codes%d" % q] = ("ac%d" % q, every)
         ev["scales%d" % q] = ("as%d" % q, every)
-    ev["fw"] = ("afw", every)
-    ev["tn"] = ("atn", every)
-    ev["hl"] = ("ah", 2 * every)
+    for name in ("fw", "tn", "t1", "ld"):
+        ev[name] = ("a" + name, every)
 
     nls = [0]
 
-    def send(src, dsts, sem, ranks):
-        ids = []
-        for q in ranks:
-            rid, pid, _ = topo.addr(T.cores[q])
-            ids.append(DstId(rid=rid, pnc=pid))
-        nls[0] += every
-        g.remote_dma_fused([RemoteDMATransfer(dst_ids=ids, dma_engine_mask=topo.mask(core, T.cores[ranks[0]]), remote_sem=T.sem[sem],
-                                              srcs=[src], dsts=dsts)], local_sem=T.sem["ls"])
+    def send(src, dst, sem, ranks):
+        nls[0] += write(g, core, T, topo, src, dst, sem, [cores[q] for q in ranks])
 
     win, scl = T["win%d" % r], T["scl%d" % r]
     v = g.vector
 
-    for k in range(4):
-        g.sync.dma_start(T.lst[16 * k:16 * k + 16, 0:12], T.ix[:]).then_inc(T.sem["lix"], 16)
-        g.scalar.dma_start(T.lst[64 + 16 * k:80 + 16 * k, 0:12], T.ix[:]).then_inc(T.sem["lix"], 16)
-    ev["ix"] = ("lix", 128)
+    did(g.sync.dma_start(T.lst[0:16, :], T.ix[:]), "lix", "ix", 16)
+    did(g.scalar.dma_start(T.lst[16:32, :], T.ix[:]), "lix", "ix", 16)
     did(g.sync.dma_start(T.wmt[:], T.wm[:]), "lwm", "wm", 16)
     did(g.sync.dma_start(T.dlt[:], T.dl[:]), "ldl", "dl", 16)
-    did(g.sync.dma_start(T.xt[:, 0:512], T.x[:, 0:512]), "lx0", "x0", 16)
-    did(g.sync.dma_start(T.xt[:, 512:2048], T.x[:, 512:2048]), "lx1", "x1", 16)
+    for k, (a, b) in enumerate(XPARTS):
+        did(g.sync.dma_start(T.xt[:, 512 * a:512 * b], T.x[:, 512 * a:512 * b]), "lx%d" % k, "x", 16)
+        for t in range(a, b):
+            ev["x%d" % t] = ev["x"]
 
     did(g.iota(T.pi[:], [[0, 2]], 0, 1), "sg", "pi")
+    did(g.iota(T.idle[:], [[32, 4]], -96, 1), "sg", "idle")
     did(g.iota(T.kk[:], [[1, CH]], 0, 0, allow_small_or_imprecise_dtypes=True), "sg", "kk")
     did(g.iota(T.c16[:], [[16, 16]], -SH, 0, allow_small_or_imprecise_dtypes=True), "sg", "c16")
     did(v.memset(T.row[:], LOW), "sv", "row")
-    did(v.memset(T.lst[:, 12:24], 0), "sv", "pad")
     after("v", "pi")
     did(v.tensor_scalar(T.qa[:], T.pi[:], 5, None, A.logical_shift_right), "sv", "qa")
     did(v.tensor_scalar(T.si[:], T.pi[:], 4, 1, A.logical_shift_right, A.bitwise_and), "sv", "si")
     did(v.tensor_scalar(T.lo[:], T.pi[:], 15, None, A.bitwise_and), "sv", "lo")
     after("v", "qa")
-    did(v.tensor_scalar(T.a64[:], T.qa[:], CH, 2 * CH, A.mult, A.min), "sv", "a64")
-    did(v.tensor_scalar(T.a4[:], T.qa[:], 4, 8, A.mult, A.min), "sv", "a4")
+    did(v.tensor_scalar(T.a64[:], T.qa[:], CH, None, A.mult), "sv", "a64")
     after("v", "si")
     did(v.tensor_scalar(T.npos[:], T.si[:], 16, -32, A.mult, A.add), "sv", "npos")
-    after("v", "lo")
-    did(v.tensor_copy(T.lof[:], T.lo[:]), "sv", "lof")
-    after("v", "a4")
-    did(v.tensor_scalar(T.sel0[:], T.lo[:], T.a4[:, 0:1], None, A.add), "sv", "sel0")
-    after("v", "npos")
-    did(v.tensor_scalar(T.selt[:], T.lo[:], 16, T.npos[:, 0:1], A.mult, A.subtract), "sv", "selt")
+    after("v", "idle")
+    did(v.tensor_copy(T.off[96:128, :], T.idle[96:128, :]), "sv", "off3")
     after("s", "kk", "a64")
     did(g.scalar.activation(T.vals[:], T.kk[:], IDENT, bias=T.a64[:, 0:1]), "ss", "vals")
-    after("s", "c16", "lof")
-    did(g.scalar.activation(T.same[:], T.c16[:], IDENT, bias=T.lof[:, 0:1]), "ss", "same")
+
+    def const_same():
+        after("v", "lo")
+        did(v.tensor_copy(T.lof[:], T.lo[:]), "sv", "lof")
+        after("s", "c16", "lof")
+        did(g.scalar.activation(T.same[:], T.c16[:], IDENT, bias=T.lof[:, 0:1]), "ss", "same")
+
+    def const_selt():
+        after("v", "lo", "npos")
+        did(v.tensor_scalar(T.selt[:], T.lo[:], 16, T.npos[:, 0:1], A.mult, A.subtract), "sv", "selt")
+
+    def offsets():
+        after("v", "ix", "npos")
+        for t in range(R):
+            did(v.tensor_scalar(T.off[32 * t:32 * t + 32, :], T.lst[0:32, 4 * t:4 * t + 4], T.npos[0:32, 0:1], None, A.subtract), "sv", "off")
+
+    def forward_lo():
+        after("v", "ix")
+        for a in (0, 32):
+            did(v.tensor_copy(T.fwo[a:a + 32, :], T.lst[0:32, 0:4]), "sv", "fwlo")
+
+    def forward():
+        after("v", "fwlo")
+        did(v.tensor_copy(T.fwo[64:128, :], T.fwo[0:64, :]), "sv", "fwo")
+        after("g", "fwo")
+        send(T.fwo[:], T.fw[:], "afw", [near])
+
+    def scatter():
+        after("v", "off3", "off", "row", "vals")
+        did(v.tensor_copy(T.row[:].indirect(T.off[:]), T.vals[:]), "sv", "scat")
+
+    def turn():
+        after("v", "scat")
+        did(v.transpose(T.tr[:], T.row[:]), "sv", "tr")
+
+    def select():
+        after("v", "tr", "selt", "same")
+        did(v.tensor_tensor(T.pp[:, 0:16], T.tr[:].indirect(T.selt[:, 0:1]), T.same[:], A.max), "sv", "m1")
+
+    def fold(t):
+        after("v", "m%d" % (t - 1))
+        a, c = 32 * (t - 1), 16 * (t - 1)
+        did(v.tensor_tensor(T.pp[0:32, c:c + 16], T.pp[0:32, c - 16:c], T.pp[a:a + 32, 0:16], A.max), "sv", "m%d" % t)
+        after("v", "m%d" % t)
+
+    def tab_lo():
+        after("v", "m3")
+        for a in (0, 32):
+            did(v.tensor_scalar(T.tab[a:a + 32, :], T.pp[0:32, :], SH, None, A.add), "sv", "tablo")
+
+    def tab_hi():
+        after("v", "tablo")
+        did(v.tensor_copy(T.tab[64:128, :], T.tab[0:64, :]), "sv", "tab")
+
+    def base():
+        after("v", "wm")
+        did(v.quantize_mx(win[:, 0:SH], scl[:, 0:SH], T.wmt[:]), "sv", "base")
+
+    def delta():
+        after("v", "dl")
+        ev["base"]
+        did(v.quantize_mx(win[:, SH:HELD], scl[:, SH:HELD], T.dlt[:]), "sv", "delta")
+        ev["codes%d" % r] = ev["scales%d" % r] = ev["delta"]
 
     def qx(t0, t1=None):
         t1 = t0 if t1 is None else t1
-        after("v", "x%d" % min(t1, 1))
+        after("v", "x%d" % t0, "x%d" % t1)
         a, b = 128 * t0, 128 * t1 + 128
         did(v.quantize_mx(T.xq[:, a:b], T.xsc[:, a:b], T.xt[:, 4 * a:4 * b]), "sv", "xq")
         for t in range(t0, t1 + 1):
             ev["xq%d" % t] = ev["xq"]
 
-    def table(q, a, b):
-        if q == r:
-            return T.tab[:, a:b], "tab"
-        if q == near:
-            return T.tn[:, a - 16:b - 16], "tn"
-        c = HALF * (peers.index(q) - 1) + (HALF if a >= HALF else 0)
-        return T.tb[:, c + a:c + b], "tb%d" % (a // HALF)
+    def send_codes(q, ranks):
+        after("g", "codes%d" % q)
+        w = T["win%d" % q][:].bitcast(dt.uint8)
+        send(w, w, "ac%d" % q, ranks)
+
+    def send_scales(q, ranks):
+        after("g", "scales%d" % q)
+        send(T["scl%d" % q][:], T["scl%d" % q][:], "as%d" % q, ranks)
+
+    def send_near_table():
+        after("g", "tab")
+        send(T.tab[:, 16:48], T.tn[:], "atn", [near])
+
+    def send_far_table():
+        after("g", "tab")
+        send(T.tab[:], T.t1[:], "at1", [far1])
+
+    def park():
+        after("y", "tablo")
+        did(g.sync.dma_start(T.td[:], T.tab[0:16, :]), "ltd", "td", 16)
+
+    def send_parked():
+        after("g", "td")
+        send(T.td[:], T.ld[:], "ald", [far2])
+
+    def repeat():
+        after("y", "ld")
+        for k in range(4):
+            did(g.sync.dma_start(T.t2[16 * k:16 * k + 16, :], T.ld[:]), "lt2", "t2lo", 16)
+
+    def repeat_more():
+        ev["t2lo"]
+        for k in range(4, 8):
+            did(g.sync.dma_start(T.t2[16 * k:16 * k + 16, :], T.ld[:]), "lt2", "t2", 16)
+
+    def repeat_hi():
+        after("v", "t2lo")
+        did(v.tensor_copy(T.t2[64:128, :], T.t2[0:64, :]), "sv", "t2")
 
     def pick(q, a, b):
-        o, e = table(q, a, b)
+        e = {r: "tab", near: "tn", far1: "t1", far2: "t2"}[q]
+        o = T.tn[:, a - 16:b - 16] if q == near else T[e][:, a:b]
         after("v", "codes%d" % q, e)
         did(v.tensor_copy(T["wc%d" % q][:, 16 * a:16 * b].bitcast(dt.uint32), T["win%d" % q][:].bitcast(dt.uint32).indirect(o)), "sv", "pc")
         after("s", "scales%d" % q, e)
         did(g.scalar.activation(T["ws%d" % q][:, 16 * a:16 * b], T["scl%d" % q][:].indirect(o), COPY), "ss", "pq")
-        for t in range(a // 16 + 1, (b - 1) // 16 + 2):
-            ev["pc%d%d" % (q, t)], ev["pq%d%d" % (q, t)] = ev["pc"], ev["pq"]
+        for j in range(a // 8, b // 8):
+            ev["pc%d_%d" % (q, j)], ev["pq%d_%d" % (q, j)] = ev["pc"], ev["pq"]
 
     bank = {}
     last = {}
 
-    def product(t, q):
+    def product(t, q, a=0, n=SH):
         b = len(bank) % 8
         after("t", "xq%d" % t)
         if b in last:
             after("t", last[b])
         plain = t == 0 or (t, q) == (1, near)
-        after("t", *(("codes%d" % q, "scales%d" % q) if plain else ("pc%d%d" % (q, t), "pq%d%d" % (q, t))))
+        c = a if plain else SH * (t - 1) + a
+        if plain:
+            after("t", "codes%d" % q, "scales%d" % q)
+        else:
+            after("t", *["p%s%d_%d" % (k, q, j) for k in "cq" for j in range(c // 128, (c + n) // 128)])
         w, sc = ("win%d", "scl%d") if plain else ("wc%d", "ws%d")
-        c = 0 if plain else SH * (t - 1)
-        n = SH + CH if plain and t else SH
+        n += CH if plain and t else 0
         x0 = 128 * t
         did(g.tensor.matmul_mx(T["ps%d" % b][:, 0:n], T.xq[:, x0:x0 + 128], T.xsc[:, x0:x0 + 128],
-                               T[w % q][:, c:c + n], T[sc % q][:, c:c + n], True, True), "st", "p%d_%d" % (t, q))
-        bank[(t, q)] = b
-        last[b] = "e%d_%d" % (t, q)
+                               T[w % q][:, c:c + n], T[sc % q][:, c:c + n], True, True), "st", "p%d_%d_%d" % (t, q, a))
+        bank[(t, q, a)] = (b, n)
+        last[b] = "e%d_%d_%d" % (t, q, a)
 
-    def copy_out(qn, out, src, name):
+    def evac(qn, t, q, a=0):
+        b, n = bank[(t, q, a)]
+        after(qn, "p%d_%d_%d" % (t, q, a))
+        dst, src, name = T["y%d%d" % (t, q)][:, a:a + n], T["ps%d" % b][:, 0:n], "e%d_%d_%d" % (t, q, a)
         if qn == "v":
-            did(v.tensor_copy(out, src), "sv", name)
+            did(v.tensor_copy(dst, src), "sv", name)
         else:
-            did(g.scalar.activation(out, src, COPY), "ss", name)
+            did(g.scalar.activation(dst, src, COPY), "ss", name)
 
-    def evac(qn, t, q):
-        c = SH * (q % 2)
-        after(qn, "p%d_%d" % (t, q))
-        ps = T["ps%d" % bank[(t, q)]]
-        if (t, q) == (1, near):
-            copy_out(qn, T.new1[:], ps[:, SH:SH + CH], "new1")
-        copy_out(qn, T["y%d%d" % (q // 2, t)][:, c:c + SH], ps[:, 0:SH], "e%d_%d" % (t, q))
-        ev["b%d_%d" % (t, q)] = ev["e%d_%d" % (t, q)]
+    def store(t, q, a=0, qn="y", done=None):
+        n = min(bank[(t, q, a)][1], SH)
+        after(qn, done or "e%d_%d_%d" % (t, q, a))
+        k = SH * (t * N + q) + a
+        did(queues[qn].dma_start(T.y[:, k:k + n], T["y%d%d" % (t, q)][:, a:a + n]), "ysem", "y", 16)
+
+    def out(qn, t, q, a=0):
+        evac(qn, t, q, a)
+        store(t, q, a)
 
     def replace():
-        c = SH * (near % 2)
-        after("v", "fwo", "new1", "e1_%d" % near)
-        did(v.tensor_copy(T["y%d1" % hh][:, c:c + SH].indirect(T.fwo[:]), T.new1[:]), "sv", "b1_%d" % near)
+        y1 = T["y1%d" % near]
+        after("v", "fw", "e1_%d_0" % near)
+        did(v.tensor_copy(y1[:, 0:SH].indirect(T.fw[:]), y1[:, SH:SH + CH]), "sv", "replaced")
+        store(1, near, done="replaced")
 
-    def store(t, h, qn="y"):
-        after(qn, "b%d_%d" % (t, 2 * h), "b%d_%d" % (t, 2 * h + 1))
-        k = SH * (t * N + 2 * h)
-        did(queues[qn].dma_start(T.y[:, k:k + 512], T["y%d%d" % (h, t)][:]), "ysem", "y", 16)
-
-    def store1(t, q, qn="y"):
-        after(qn, "b%d_%d" % (t, q))
-        k, c = SH * (t * N + q), SH * (q % 2)
-        did(queues[qn].dma_start(T.y[:, k:k + SH], T["y%d%d" % (q // 2, t)][:, c:c + SH]), "ysem", "y", 16)
-
-    def out(qn, t, q):
-        evac(qn, t, q)
-        store1(t, q)
-
-    def spread(k):
-        after("v", "hl")
-        for a in (0, 64):
-            did(v.tensor_scalar(T.tb[a:a + 64, 2 * HALF * k:2 * HALF * (k + 1)], T.hl[64 * k:64 * k + 64, :], SH, None, A.add), "sv", "tb%d" % k)
-
-    after("g", "ix")
-    send(T.lst[:, 0:4], [T.fw[:]], "afw", [near])
-
-    after("v", "ix", "pad", "sel0", "npos")
-    did(v.tensor_scalar(T.off[:], T.lst[:].indirect(T.sel0[:, 0:1]), T.npos[:, 0:1], None, A.subtract), "sv", "off")
-    after("v", "off", "row", "vals")
-    did(v.tensor_copy(T.row[:].indirect(T.off[:, 0:4]), T.vals[:]), "sv", "scat")
-    after("v", "wm")
-    did(v.quantize_mx(win[:, 0:SH], scl[:, 0:SH], T.wmt[:]), "sv", "base")
-    after("v", "scat")
-    did(v.transpose(T.tr[:], T.row[:]), "sv", "tr")
-    after("v", "dl")
-    did(v.quantize_mx(win[:, SH:HELD], scl[:, SH:HELD], T.dlt[:]), "sv", "delta")
-    ev["codes%d" % r] = ev["scales%d" % r] = ev["delta"]
-    after("v", "tr", "selt", "same")
-    did(v.tensor_tensor(T.pp[:, 0:16], T.tr[:].indirect(T.selt[:, 0:1]), T.same[:], A.max), "sv", "q")
-    qx(0)
-    product(0, r)
-    after("v", "q")
-    did(v.tensor_tensor(T.pp[0:32, 16:32], T.pp[0:32, 0:16], T.pp[32:64, 0:16], A.max), "sv", "m2")
-    after("v", "m2")
-    did(v.tensor_tensor(T.pp[0:32, 32:48], T.pp[0:32, 16:32], T.pp[64:96, 0:16], A.max), "sv", "m3")
-    after("v", "m3")
-    for a in range(0, 128, 32):
-        did(v.tensor_scalar(T.tab[a:a + 32, :], T.pp[0:32, :], SH, None, A.add), "sv", "tab")
-
-    def halves():
-        for a in range(0, 128, 32):
-            c = HALF * (a // 64)
-            after("s", "m3")
-            did(g.scalar.activation(T.half[a:a + 32, :], T.pp[0:32, c:c + HALF], COPY), "ss", "half")
-
-    halves()
-    evac("s", 0, r)
-    qx(1)
-    pick(r, 0, 16)
-
-    codes = win[:].bitcast(dt.uint8)
-    after("g", "delta")
-    send(codes, [codes], "ac%d" % r, [near])
-    send(scl[:], [scl[:]] * 3, "as%d" % r, peers)
-    after("g", "half")
-    send(T.half[:], [T.hl[:, 0:HALF], T.hl[:, HALF:2 * HALF]], "ah", [far1, far2])
-    after("g", "tab")
-    send(T.tab[:, 16:48], [T.tn[:]], "atn", [near])
-    send(codes, [codes], "ac%d" % r, [far1])
-    send(codes, [codes], "ac%d" % r, [far2])
-
-    product(1, r)
-    qx(2, 3)
-    pick(r, 16, 32)
-    product(2, r)
-    pick(r, 32, 48)
-    product(3, r)
-    after("v", "fw")
-    did(v.tensor_copy(T.fwo[:], T.fw[:]), "sv", "fwo")
-    out("v", 1, r)
-    store1(0, r)
-    out("s", 2, r)
-    product(0, near)
-    product(1, near)
-    pick(near, 16, 48)
-    out("v", 3, r)
-    evac("s", 1, near)
-    out("s", 0, near)
-    product(2, near)
-    product(3, near)
-    spread(0)
-    pick(far1, 0, 24)
-    replace()
-    store1(1, near)
-    out("v", 2, near)
-    out("s", 3, near)
-    product(0, far1)
-    product(1, far1)
-    spread(1)
-    pick(far2, 0, 24)
-    product(0, far2)
-    product(1, far2)
-    out("s", 0, far1)
-    out("v", 1, far1)
-    pick(far1, 24, 48)
-    product(2, far1)
-    product(3, far1)
-    out("s", 0, far2)
-    out("s", 1, far2)
-    pick(far2, 24, 32)
-    product(2, far2)
-    pick(far2, 32, 48)
-    product(3, far2)
-    out("v", 2, far1)
-    out("v", 3, far1)
-    out("s", 2, far2)
-    out("v", 3, far2)
+    const_same();const_selt();forward_lo();offsets();forward();scatter();base();turn();delta();select();qx(0);product(0,r);fold(2);fold(3);tab_lo();park();qx(1);tab_hi()
+    send_codes(r,[near]);send_scales(r,[near,far1]);send_near_table();send_codes(r,[far1]);send_far_table();send_parked();send_scales(far1,[near]);send_codes(far1,[near])
+    evac("s",0,r);pick(r,0,16);product(1,r);qx(2,3);pick(r,16,48);product(1,near);product(0,near);out("s",1,r);store(0,r);out("s",0,near);evac("v",1,near)
+    product(2,r);product(3,r);pick(near,16,48);repeat();repeat_more();replace();out("s",2,r);out("s",3,r)
+    pick(far1,0,32);product(2,near);product(3,near);product(0,far1);product(1,far1);out("v",2,near);out("v",3,near);out("s",0,far1);product(2,far1)
+    pick(far1,32,48);out("v",1,far1);out("s",2,far1);product(0,far2);product(3,far1)
+    pick(far2,0,32);product(1,far2);out("v",3,far1);out("s",0,far2);product(2,far2);pick(far2,32,48);out("v",1,far2);out("s",2,far2);product(3,far2);out("v",3,far2)
 
     g.wait_ge(T.sem["ls"], nls[0])
     after("y", "y")

from concourse.bass import DstId, RemoteDMATransfer
from concourse.mybir import dt, AluOpType, ActivationFunctionType

N, SH, CH, R = 4, 256, 64, 3
NEW = R * CH
HELD = SH + NEW
SEG = SH + 32
LOW = -8192.0
XPARTS = [(0, 1), (1, 2), (2, 4)]

SCRATCH = {
    "wmt": ("sbuf", [128, 4 * SH], "bfloat16"),
    "dlt": ("sbuf", [128, 4 * NEW], "bfloat16"),
    "xt": ("sbuf", [128, 512 * (R + 1)], "bfloat16"),
    "xq": ("sbuf", [128, 512], "float8_e4m3fn_x4"),
    "xsc": ("sbuf", [128, 512], "uint8"),
    "lst": ("sbuf", [128, 12], "int32"),
    "idle": ("sbuf", [128, 4], "int32"),
    "off": ("sbuf", [128, 4], "uint16"),
    "vals": ("sbuf", [128, CH], "bfloat16"),
    "row": ("sbuf", [128, SEG], "bfloat16"),
    "tr": ("sbuf", [128, SEG], "bfloat16"),
    "pi": ("sbuf", [128, 2], "int32"),
    "kk": ("sbuf", [128, CH], "float32"),
    "c16": ("sbuf", [128, 16], "float32"),
    "same": ("sbuf", [128, 16], "float32"),
    "si": ("sbuf", [128, 2], "int32"),
    "qa": ("sbuf", [128, 2], "int32"),
    "lo": ("sbuf", [128, 2], "int32"),
    "lof": ("sbuf", [128, 2], "float32"),
    "npos": ("sbuf", [128, 2], "float32"),
    "a64": ("sbuf", [128, 2], "float32"),
    "selt": ("sbuf", [128, 2], "uint16"),
    "pp": ("sbuf", [128, 48], "float32"),
    "tab": ("sbuf", [128, 48], "uint16"),
    "tn": ("sbuf", [128, 32], "uint16"),
    "t1": ("sbuf", [128, 48], "uint16"),
    "t2": ("sbuf", [128, 48], "uint16"),
    "td": ("dram", [128, 6], "uint16"),
    "ld": ("dram", [128, 6], "uint16"),
    "fwo": ("sbuf", [128, 4], "uint16"),
    "fw": ("sbuf", [128, 4], "uint16"),
}
for _q in range(N):
    SCRATCH["win%d" % _q] = ("sbuf", [128, HELD], "float8_e4m3fn_x4")
    SCRATCH["scl%d" % _q] = ("sbuf", [128, HELD], "uint8")
    SCRATCH["wc%d" % _q] = ("sbuf", [128, R * SH], "float8_e4m3fn_x4")
    SCRATCH["ws%d" % _q] = ("sbuf", [128, R * SH], "uint8")
    for _t in range(R + 1):
        SCRATCH["y%d%d" % (_t, _q)] = ("sbuf", [128, SH + CH * (_t == 1)], "float32")
for _b in range(8):
    SCRATCH["ps%d" % _b] = ("psum", [128, 512], "float32")

SEMAPHORES = ["sv", "ss", "st", "sg", "lix", "lwm", "ldl", "lx0", "lx1", "lx2", "ltd", "lt2", "ysem", "ls", "afw", "atn", "at1", "ald"]
for _q in range(N):
    SEMAPHORES += ["ac%d" % _q, "as%d" % _q]


def places(q, T, topo):
    die = topo.die(T.cores[q])
    mine = [p for p in range(N) if topo.die(T.cores[p]) == die]
    other = [p for p in range(N) if p not in mine]
    spare = [c for c in topo.cores_of(T.cores[q]) if T.rank_of(c) is None and topo.die(c) != die]
    i = mine.index(q)
    return mine[1 - i], other[i], other[1 - i], spare[i]


def write(g, core, T, topo, src, dst, sem, cores):
    ids = []
    for c in cores:
        rid, pid, _ = topo.addr(c)
        ids.append(DstId(rid=rid, pnc=pid))
    g.remote_dma_fused([RemoteDMATransfer(dst_ids=ids, dma_engine_mask=topo.mask(core, cores[0]), remote_sem=T.sem[sem],
                                          srcs=[src], dsts=[dst for _ in cores])], local_sem=T.sem["ls"])
    return len(topo.engines(core, cores[0]))


def hand_on(g, core, T, topo):
    for q in range(N):
        _, far1, far2, spare = places(q, T, topo)
        if spare == core and HELP:
            sent = 0
            for sem, w in (("as%d" % q, T["scl%d" % q][:]), ("ac%d" % q, T["win%d" % q][:].bitcast(dt.uint8))):
                g.wait_ge(T.sem[sem], len(topo.engines(T.cores[q], core)))
                sent += write(g, core, T, topo, w, w, sem, [T.cores[far1], T.cores[far2]])
            g.wait_ge(T.sem["ls"], sent)


HELP = False


def rank_program(g, core, T, topo):
    r = T.rank_of(core)
    if r is None:
        hand_on(g, core, T, topo)
        return
    A = AluOpType
    COPY = ActivationFunctionType.Copy
    IDENT = ActivationFunctionType.Identity
    queues = {"v": g.vector, "s": g.scalar, "t": g.tensor, "g": g, "y": g.sync}
    count = {}
    ev = {}
    seen = {}

    def after(qn, *names):
        for n in names:
            sem, val = ev[n]
            if seen.get((qn, sem), 0) < val:
                queues[qn].wait_ge(T.sem[sem], val)
                seen[(qn, sem)] = val

    def did(ins, sem, name, n=1):
        count[sem] = count.get(sem, 0) + n
        ins.then_inc(T.sem[sem], n)
        ev[name] = (sem, count[sem])

    near, far1, far2, spare = places(r, T, topo)
    cores = list(T.cores) + [spare]
    H = N
    every = len(topo.engines(core, T.cores[near]))
    for q in (near, far1, far2):
        ev["codes%d" % q] = ("ac%d" % q, every)
        ev["scales%d" % q] = ("as%d" % q, every)
    for name in ("fw", "tn", "t1", "ld"):
        ev[name] = ("a" + name, every)

    nls = [0]

    def send(src, dst, sem, ranks):
        nls[0] += write(g, core, T, topo, src, dst, sem, [cores[q] for q in ranks])

    win, scl = T["win%d" % r], T["scl%d" % r]
    v = g.vector

    did(g.sync.dma_start(T.lst[0:16, :], T.ix[:]), "lix", "ix", 16)
    did(g.scalar.dma_start(T.lst[16:32, :], T.ix[:]), "lix", "ix", 16)
    did(g.sync.dma_start(T.wmt[:], T.wm[:]), "lwm", "wm", 16)
    did(g.sync.dma_start(T.dlt[:], T.dl[:]), "ldl", "dl", 16)
    for k, (a, b) in enumerate(XPARTS):
        did(g.sync.dma_start(T.xt[:, 512 * a:512 * b], T.x[:, 512 * a:512 * b]), "lx%d" % k, "x", 16)
        for t in range(a, b):
            ev["x%d" % t] = ev["x"]

    did(g.iota(T.pi[:], [[0, 2]], 0, 1), "sg", "pi")
    did(g.iota(T.idle[:], [[32, 4]], -96, 1), "sg", "idle")
    did(g.iota(T.kk[:], [[1, CH]], 0, 0, allow_small_or_imprecise_dtypes=True), "sg", "kk")
    did(g.iota(T.c16[:], [[16, 16]], -SH, 0, allow_small_or_imprecise_dtypes=True), "sg", "c16")
    did(v.memset(T.row[:], LOW), "sv", "row")
    after("v", "pi")
    did(v.tensor_scalar(T.qa[:], T.pi[:], 5, None, A.logical_shift_right), "sv", "qa")
    did(v.tensor_scalar(T.si[:], T.pi[:], 4, 1, A.logical_shift_right, A.bitwise_and), "sv", "si")
    did(v.tensor_scalar(T.lo[:], T.pi[:], 15, None, A.bitwise_and), "sv", "lo")
    after("v", "qa")
    did(v.tensor_scalar(T.a64[:], T.qa[:], CH, None, A.mult), "sv", "a64")
    after("v", "si")
    did(v.tensor_scalar(T.npos[:], T.si[:], 16, -32, A.mult, A.add), "sv", "npos")
    after("v", "idle")
    did(v.tensor_copy(T.off[96:128, :], T.idle[96:128, :]), "sv", "off3")
    after("s", "kk", "a64")
    did(g.scalar.activation(T.vals[:], T.kk[:], IDENT, bias=T.a64[:, 0:1]), "ss", "vals")

    def const_same():
        after("v", "lo")
        did(v.tensor_copy(T.lof[:], T.lo[:]), "sv", "lof")
        after("s", "c16", "lof")
        did(g.scalar.activation(T.same[:], T.c16[:], IDENT, bias=T.lof[:, 0:1]), "ss", "same")

    def const_selt():
        after("v", "lo", "npos")
        did(v.tensor_scalar(T.selt[:], T.lo[:], 16, T.npos[:, 0:1], A.mult, A.subtract), "sv", "selt")

    def offsets():
        after("v", "ix", "npos")
        for t in range(R):
            did(v.tensor_scalar(T.off[32 * t:32 * t + 32, :], T.lst[0:32, 4 * t:4 * t + 4], T.npos[0:32, 0:1], None, A.subtract), "sv", "off")

    def forward_lo():
        after("v", "ix")
        for a in (0, 32):
            did(v.tensor_copy(T.fwo[a:a + 32, :], T.lst[0:32, 0:4]), "sv", "fwlo")

    def forward():
        after("v", "fwlo")
        did(v.tensor_copy(T.fwo[64:128, :], T.fwo[0:64, :]), "sv", "fwo")
        after("g", "fwo")
        send(T.fwo[:], T.fw[:], "afw", [near])

    def scatter():
        after("v", "off3", "off", "row", "vals")
        did(v.tensor_copy(T.row[:].indirect(T.off[:]), T.vals[:]), "sv", "scat")

    def turn():
        after("v", "scat")
        did(v.transpose(T.tr[:], T.row[:]), "sv", "tr")

    def select():
        after("v", "tr", "selt", "same")
        did(v.tensor_tensor(T.pp[:, 0:16], T.tr[:].indirect(T.selt[:, 0:1]), T.same[:], A.max), "sv", "m1")

    def fold(t):
        after("v", "m%d" % (t - 1))
        a, c = 32 * (t - 1), 16 * (t - 1)
        did(v.tensor_tensor(T.pp[0:32, c:c + 16], T.pp[0:32, c - 16:c], T.pp[a:a + 32, 0:16], A.max), "sv", "m%d" % t)
        after("v", "m%d" % t)

    def tab_lo():
        after("v", "m3")
        for a in (0, 32):
            did(v.tensor_scalar(T.tab[a:a + 32, :], T.pp[0:32, :], SH, None, A.add), "sv", "tablo")

    def tab_hi():
        after("v", "tablo")
        did(v.tensor_copy(T.tab[64:128, :], T.tab[0:64, :]), "sv", "tab")

    def base():
        after("v", "wm")
        did(v.quantize_mx(win[:, 0:SH], scl[:, 0:SH], T.wmt[:]), "sv", "base")

    def delta():
        after("v", "dl")
        ev["base"]
        did(v.quantize_mx(win[:, SH:HELD], scl[:, SH:HELD], T.dlt[:]), "sv", "delta")
        ev["codes%d" % r] = ev["scales%d" % r] = ev["delta"]

    def qx(t0, t1=None):
        t1 = t0 if t1 is None else t1
        after("v", "x%d" % t0, "x%d" % t1)
        a, b = 128 * t0, 128 * t1 + 128
        did(v.quantize_mx(T.xq[:, a:b], T.xsc[:, a:b], T.xt[:, 4 * a:4 * b]), "sv", "xq")
        for t in range(t0, t1 + 1):
            ev["xq%d" % t] = ev["xq"]

    def send_codes(q, ranks):
        after("g", "codes%d" % q)
        w = T["win%d" % q][:].bitcast(dt.uint8)
        send(w, w, "ac%d" % q, ranks)

    def send_scales(q, ranks):
        after("g", "scales%d" % q)
        send(T["scl%d" % q][:], T["scl%d" % q][:], "as%d" % q, ranks)

    def send_near_table():
        after("g", "tab")
        send(T.tab[:, 16:48], T.tn[:], "atn", [near])

    def send_far_table():
        after("g", "tab")
        send(T.tab[:], T.t1[:], "at1", [far1])

    def park():
        after("y", "tablo")
        did(g.sync.dma_start(T.td[:], T.tab[0:16, :]), "ltd", "td", 16)

    def send_parked():
        after("g", "td")
        send(T.td[:], T.ld[:], "ald", [far2])

    def repeat():
        after("y", "ld")
        for k in range(4):
            did(g.sync.dma_start(T.t2[16 * k:16 * k + 16, :], T.ld[:]), "lt2", "t2lo", 16)

    def repeat_more():
        ev["t2lo"]
        for k in range(4, 8):
            did(g.sync.dma_start(T.t2[16 * k:16 * k + 16, :], T.ld[:]), "lt2", "t2", 16)

    def repeat_hi():
        after("v", "t2lo")
        did(v.tensor_copy(T.t2[64:128, :], T.t2[0:64, :]), "sv", "t2")

    def pick(q, a, b):
        e = {r: "tab", near: "tn", far1: "t1", far2: "t2"}[q]
        o = T.tn[:, a - 16:b - 16] if q == near else T[e][:, a:b]
        after("v", "codes%d" % q, e)
        did(v.tensor_copy(T["wc%d" % q][:, 16 * a:16 * b].bitcast(dt.uint32), T["win%d" % q][:].bitcast(dt.uint32).indirect(o)), "sv", "pc")
        after("s", "scales%d" % q, e)
        did(g.scalar.activation(T["ws%d" % q][:, 16 * a:16 * b], T["scl%d" % q][:].indirect(o), COPY), "ss", "pq")
        for j in range(a // 8, b // 8):
            ev["pc%d_%d" % (q, j)], ev["pq%d_%d" % (q, j)] = ev["pc"], ev["pq"]

    bank = {}
    last = {}

    def product(t, q, a=0, n=SH):
        b = len(bank) % 8
        after("t", "xq%d" % t)
        if b in last:
            after("t", last[b])
        plain = t == 0 or (t, q) == (1, near)
        c = a if plain else SH * (t - 1) + a
        if plain:
            after("t", "codes%d" % q, "scales%d" % q)
        else:
            after("t", *["p%s%d_%d" % (k, q, j) for k in "cq" for j in range(c // 128, (c + n) // 128)])
        w, sc = ("win%d", "scl%d") if plain else ("wc%d", "ws%d")
        n += CH if plain and t else 0
        x0 = 128 * t
        did(g.tensor.matmul_mx(T["ps%d" % b][:, 0:n], T.xq[:, x0:x0 + 128], T.xsc[:, x0:x0 + 128],
                               T[w % q][:, c:c + n], T[sc % q][:, c:c + n], True, True), "st", "p%d_%d_%d" % (t, q, a))
        bank[(t, q, a)] = (b, n)
        last[b] = "e%d_%d_%d" % (t, q, a)

    def evac(qn, t, q, a=0):
        b, n = bank[(t, q, a)]
        after(qn, "p%d_%d_%d" % (t, q, a))
        dst, src, name = T["y%d%d" % (t, q)][:, a:a + n], T["ps%d" % b][:, 0:n], "e%d_%d_%d" % (t, q, a)
        if qn == "v":
            did(v.tensor_copy(dst, src), "sv", name)
        else:
            did(g.scalar.activation(dst, src, COPY), "ss", name)

    def store(t, q, a=0, qn="y", done=None):
        n = min(bank[(t, q, a)][1], SH)
        after(qn, done or "e%d_%d_%d" % (t, q, a))
        k = SH * (t * N + q) + a
        did(queues[qn].dma_start(T.y[:, k:k + n], T["y%d%d" % (t, q)][:, a:a + n]), "ysem", "y", 16)

    def out(qn, t, q, a=0):
        evac(qn, t, q, a)
        store(t, q, a)

    def replace():
        y1 = T["y1%d" % near]
        after("v", "fw", "e1_%d_0" % near)
        did(v.tensor_copy(y1[:, 0:SH].indirect(T.fw[:]), y1[:, SH:SH + CH]), "sv", "replaced")
        store(1, near, done="replaced")

    const_same();const_selt();forward_lo();offsets();forward();scatter();base();turn();delta();select();qx(0);product(0,r);fold(2);fold(3);tab_lo();park();qx(1);tab_hi()
    send_codes(r,[near]);send_scales(r,[near,far1]);send_near_table();send_codes(r,[far1]);send_far_table();send_parked();send_scales(far1,[near]);send_codes(far1,[near])
    evac("s",0,r);pick(r,0,16);product(1,r);qx(2,3);pick(r,16,48);product(1,near);product(0,near);out("s",1,r);store(0,r);out("s",0,near);evac("v",1,near)
    product(2,r);product(3,r);pick(near,16,48);repeat();repeat_more();replace();out("s",2,r);out("s",3,r)
    pick(far1,0,32);product(2,near);product(3,near);product(0,far1);product(1,far1);out("v",2,near);out("v",3,near);out("s",0,far1);product(2,far1)
    pick(far1,32,48);out("v",1,far1);out("s",2,far1);product(0,far2);product(3,far1)
    pick(far2,0,32);product(1,far2);out("v",3,far1);out("s",0,far2);product(2,far2);pick(far2,32,48);out("v",1,far2);out("s",2,far2);product(3,far2);out("v",3,far2)

    g.wait_ge(T.sem["ls"], nls[0])
    after("y", "y")
